import numpy as np
import ml_dtypes


def mxq(x, axis, fmt="e4m3"):
    dtype, down = {"e4m3": (ml_dtypes.float8_e4m3fn, 7), "e5m2": (ml_dtypes.float8_e5m2, 14)}[fmt]
    v = np.moveaxis(np.asarray(x, np.float32).astype(ml_dtypes.bfloat16).astype(np.float64), axis, -1)
    blocks = v.reshape(v.shape[:-1] + (-1, 32))
    amax = np.abs(blocks).max(-1, keepdims=True)
    byte = np.maximum(np.where(amax > 0, np.frexp(amax)[1] - 1 + 127, 0) - down, 1)
    scale = np.exp2(byte - 127.0)
    codes = (blocks / scale).astype(np.float32).astype(dtype).astype(np.float64)
    return np.moveaxis((codes * scale).reshape(v.shape), -1, axis)


WIDE = False


def mx_kscale(k):
    if not WIDE:
        return np.ones(k)
    levels = np.array([10, -10, 5, -5, 0])
    if k % 512:
        return np.exp2(np.random.permutation(np.resize(levels, k // 32))).repeat(32)
    a = np.empty((k // 512, 16))
    for p in range(k // 512):
        a[p, :8] = np.random.permutation(np.resize(levels, 8))
        for g in range(8):
            far = levels[np.abs(levels - a[p, g]) >= 10]
            a[p, g + 8] = far[np.random.randint(len(far))]
    return np.exp2(a.ravel()).repeat(32)


def f64(x):
    return np.asarray(x).astype(np.float64)


def striped(idx):
    return np.tile(idx.reshape(-1, 16).T, (8, 1)).astype(np.uint16)


def unstriped(offs):
    return offs[:16].T.reshape(-1).astype(np.int64)


E2M1 = np.array([0.0, 0.5, 1.0, 1.5, 2.0, 3.0, 4.0, 6.0, -0.0, -0.5, -1.0, -1.5, -2.0, -3.0, -4.0, -6.0])


def pack_weight(w, fmt):
    k, n = w.shape
    w = f64(np.asarray(w, np.float32).astype(ml_dtypes.bfloat16)).reshape(k // 32, 32, n)
    amax = np.abs(w).max(1)
    if fmt == "e4m3":
        byte = np.frexp(amax)[1] - 1 + 127 - 7
    else:
        mant, ex = np.frexp(amax / 6.0)
        byte = np.where(mant > 0.5, ex, ex - 1) + 127
    byte = np.clip(np.where(amax > 0, byte, 1), 1, 254)
    scaled = (w * np.exp2(127.0 - byte)[:, None, :]).reshape(k, n).astype(np.float32)
    by_word = np.ascontiguousarray(scaled.reshape(k // 512, 128, 4, n).transpose(0, 1, 3, 2))
    if fmt == "e4m3":
        words = by_word.astype(ml_dtypes.float8_e4m3fn).view(np.uint8)
    else:
        c = by_word.astype(ml_dtypes.float4_e2m1fn).view(np.uint8) & 0xF
        words = (c[..., 0::2] | (c[..., 1::2] << 4)).reshape(k // 512, 128, 2 * n)
    return np.ascontiguousarray(words), np.ascontiguousarray(byte.astype(np.uint8).reshape(k // 512, 16, n))


def unpack_weight(words, scales, fmt):
    g, _, n = scales.shape
    words = np.ascontiguousarray(words).reshape(g, 128, n, -1)
    if fmt == "e4m3":
        vals = words.view(ml_dtypes.float8_e4m3fn).astype(np.float64)
    else:
        nib = np.empty((g, 128, n, 4), np.uint8)
        nib[..., 0::2] = words & 0xF
        nib[..., 1::2] = words >> 4
        vals = E2M1[nib]
    vals = vals * np.repeat(np.exp2(scales.astype(np.float64) - 127.0), 8, axis=1)[..., None]
    return vals.transpose(0, 1, 3, 2).reshape(g * 512, n)


def gelu(v):
    return 0.5 * v * (1.0 + np.tanh(np.sqrt(2.0 / np.pi) * (v + 0.044715 * v**3)))


K, KA, KB, H, T, S, P = 1536, 1024, 512, 1024, 4096, 1024, 512

def setup_inputs():
    n = np.random.standard_normal
    s = mx_kscale(K)[:, None]
    u = mx_kscale(H)
    tab_words, tab_scales = pack_weight(n((K, T)) * s, "e4m3")
    w4_words, w4_scales = pack_weight(n((KB, H)) * 1.3 / np.sqrt(K) / s[KA:], "e2m1")
    return {
        "tab_words": tab_words, "tab_scales": tab_scales,
        "offs": striped(np.random.permutation(T)[:S]),
        "pos1": striped(np.random.permutation(S)[:P]),
        "pos2": striped(np.random.permutation(S)[:P]),
        "w1": (n((KA, H)) * 1.3 / np.sqrt(K) / s[:KA]).astype(np.float32),
        "w4_words": w4_words, "w4_scales": w4_scales,
        "gain": (np.exp(0.3 * n(H)) * u).astype(np.float32),
        "slope": (0.6 * n(H)).astype(np.float32),
        "mix": (4.5 * n(H) / np.sqrt(H) / u ** 2).astype(np.float32),
        "row": (0.8 * n(P)).astype(np.float32),
        "col": (1.5 * np.exp(0.4 * n(P))).astype(np.float32),
    }

def reference(tab_words, tab_scales, offs, pos1, pos2, w1, w4_words, w4_scales, gain, slope, mix, row, col):
    v = unpack_weight(tab_words, tab_scales, "e4m3")[:, unstriped(offs)]
    w4 = unpack_weight(w4_words, w4_scales, "e2m1")
    f = mxq(f64(w1), 0, "e4m3").T @ v[:KA] + w4.T @ v[KA:]
    h = f64(gain)[:, None] * np.tanh(f)
    x1 = h[:, unstriped(pos1)]
    go = h[:, unstriped(pos2)]
    x2 = np.maximum(go, f64(slope)[:, None] * go) * f64(mix)[:, None]
    e = mxq(x1, 0, "e4m3").T @ mxq(x2, 0, "e4m3")
    return f64(col)[:, None] / (1.0 + np.exp(-(e + f64(row)[None, :])))

@@ -1,0 +1,321 @@
+from contextlib import ExitStack
+
+import concourse.mybir as mybir
+
+F32 = mybir.dt.float32
+BF16 = mybir.dt.bfloat16
+I32 = mybir.dt.int32
+U32 = mybir.dt.uint32
+U16 = mybir.dt.uint16
+U8 = mybir.dt.uint8
+FP8X4 = mybir.dt.float8_e4m3fn_x4
+FP4X4 = mybir.dt.float4_e2m1fn_x4
+ALU = mybir.AluOpType
+ACT = mybir.ActivationFunctionType
+
+P = 128
+PACK = 4
+KP = 512
+T = 4096
+S = 1024
+H = 1024
+NP = 512
+NB = 512
+FLOPS = 2 * 1536 * H * S + 2 * H * NP * NP
+SCALE_ROW = (4, 8, 0)
+
+
+def tile_list_baton_exchange_scores_kernel(
+    tc, tab_words, tab_scales, offs, pos1, pos2, w1, w4_words, w4_scales, gain, slope, mix, row, col, out
+):
+    nc = tc.nc
+    with ExitStack() as ctx:
+        keep = ctx.enter_context(tc.tile_pool(name="keep", bufs=1))
+        ring = ctx.enter_context(tc.tile_pool(name="ring", bufs=2))
+        hpool = ctx.enter_context(tc.tile_pool(name="hpool", bufs=4))
+        psum = ctx.enter_context(tc.psum_pool(name="psum", bufs=1))
+
+        offs_sb = keep.tile([P, S // 16], U16, name="offs_sb")
+        pos1_sb = keep.tile([P, NP // 16], U16, name="pos1_sb")
+        pos2_sb = keep.tile([P, NP // 16], U16, name="pos2_sb")
+        tab_sb = [keep.tile([P, T], U32, name=f"tab_sb{a}", align_bytes=64) for a in range(3)]
+        tabsc_sb = keep.tile([P, T], U8, name="tabsc_sb", align_bytes=64)
+        w4_raw = keep.tile([P, 2 * H], U8, name="w4_raw", align_bytes=64)
+        w4sc_raw = keep.tile([P, H], U8, name="w4sc_raw", align_bytes=64)
+        gain_sb = keep.tile([P, 2, PACK], F32, name="gain_sb")
+        slope_sb = keep.tile([P, 2, PACK], F32, name="slope_sb")
+        mix_sb = keep.tile([P, 2, PACK], F32, name="mix_sb")
+        row_sb = keep.tile([P, NP], F32, name="row_sb")
+        col_sb = keep.tile([P, NP // P], F32, name="col_sb")
+
+        def load_tab(a):
+            nc.sync.dma_start(
+                out=tab_sb[a][:].bitcast(I32), in_=tab_words[a].rearrange("p n t -> p (n t)").bitcast(I32)
+            )
+
+        w1_raw = {}
+
+        def load_w1(a, b, c0, c1):
+            raw = keep.tile([P, PACK, c1 - c0], F32, name=f"w1_raw{(a + b) % 2}{b * (1 - a)}_{c0}")
+            w1_raw[a, b, c0] = raw
+            rows = w1[KP * a : KP * (a + 1), KP * b + c0 : KP * b + c1]
+            nc.sync.dma_start(out=raw[:], in_=rows.rearrange("(p j) c -> p j c", j=PACK))
+
+        nc.vector.memset(tabsc_sb[:].bitcast(I32), 0)
+        nc.vector.memset(w4sc_raw[:].bitcast(I32), 0)
+
+        nc.sync.dma_start(offs_sb[:], offs)
+        load_tab(2)
+        for vec_sb, vec in ((gain_sb, gain), (mix_sb, mix), (slope_sb, slope)):
+            nc.scalar.dma_start(out=vec_sb[:], in_=vec.rearrange("(b p t) -> p b t", p=P, t=PACK))
+        nc.sync.dma_start(out=w4_raw[:].bitcast(I32), in_=w4_words[0].bitcast(I32))
+        load_tab(0)
+        load_w1(0, 0, 0, KP)
+        load_tab(1)
+        nc.sync.dma_start(pos1_sb[:], pos1)
+        nc.sync.dma_start(pos2_sb[:], pos2)
+        load_w1(1, 0, 0, KP // 2)
+        load_w1(1, 0, KP // 2, KP)
+        load_w1(0, 1, 0, KP)
+        load_w1(1, 1, 0, KP)
+        nc.sync.dma_start(out=row_sb[:], in_=row.partition_broadcast(P))
+        with nc.allow_non_contiguous_dma(reason="one factor for each output row"):
+            nc.sync.dma_start(out=col_sb[:], in_=col.rearrange("(i p) -> p i", p=P))
+
+        for q in range(4):
+            nc.gpsimd.dma_start(
+                out=tabsc_sb[32 * q : 32 * q + 4, :].bitcast(I32),
+                in_=tab_scales[2, 4 * q : 4 * q + 4, :].bitcast(I32),
+            )
+            nc.gpsimd.dma_start(
+                out=tabsc_sb[32 * q + 4 : 32 * q + 12, :].bitcast(I32),
+                in_=tab_scales[0:2, 4 * q : 4 * q + 4, :].bitcast(I32),
+            )
+        for q in range(4):
+            nc.gpsimd.dma_start(
+                out=w4sc_raw[32 * q : 32 * q + 4, :].bitcast(I32),
+                in_=w4_scales[0, 4 * q : 4 * q + 4, :].bitcast(I32),
+            )
+
+        sign = keep.tile([P, 2, PACK], F32, name="sign")
+        fac1 = keep.tile([P, 2, PACK], F32, name="fac1")
+        fac2 = keep.tile([P, 2, PACK], F32, name="fac2")
+        nc.vector.tensor_scalar(sign[:], mix_sb[:], 0.0, None, ALU.is_ge)
+        nc.vector.tensor_scalar(sign[:], sign[:], 2.0, -1.0, ALU.mult, ALU.add)
+        nc.vector.tensor_tensor(fac1[:], gain_sb[:], sign[:], ALU.mult)
+        nc.vector.tensor_tensor(fac2[:], fac1[:], mix_sb[:], ALU.mult)
+        wide1 = [keep.tile([P, PACK, NP], F32, name=f"wide1_{b}") for b in range(2)]
+        wide2 = [keep.tile([P, PACK, NP], F32, name=f"wide2_{b}", align_bytes=64) for b in range(2)]
+        for b in range(2):
+            for wide, fac in ((wide2, fac2), (wide1, fac1)):
+                nc.scalar.copy(wide[b][:], fac[:, b, :].unsqueeze(2).to_broadcast([P, PACK, NP]))
+
+        v_words = {}
+        v_scales = keep.tile([P, S], U8, name="v_scales", align_bytes=64)
+
+        def gather_tab(a):
+            tag = ("tabsc_sb", "w4sc_raw", "v_words2")[a]
+            v_words[a] = keep.tile([P, S], U32, name=f"v_words{a}", tag=tag, align_bytes=64)
+            nc.vector.tensor_copy(v_words[a][:], tab_sb[a][:].indirect(offs_sb[:]))
+
+        w4_codes = keep.tile([P, 2 * H], U8, name="w4_codes", align_bytes=64)
+        w4_sc = keep.tile([P, H], U8, name="w4_sc", align_bytes=64)
+        gather_tab(2)
+        nc.vector.tensor_copy(
+            w4_codes[:].rearrange("p (b t m e) -> p b t m e", b=2, t=PACK, e=2),
+            w4_raw[:].rearrange("p (b m t e) -> p b t m e", b=2, t=PACK, e=2),
+        )
+        nc.vector.tensor_copy(v_scales[:], tabsc_sb[:].indirect(offs_sb[:]))
+        nc.vector.tensor_copy(
+            w4_sc[:].rearrange("p (b t m) -> p b t m", b=2, t=PACK),
+            w4sc_raw[:].rearrange("p (b m t) -> p b t m", b=2, t=PACK),
+        )
+
+        w1_codes = {}
+        w1_sc = {}
+        w1_stage = {}
+
+        def new_w1(a, b):
+            w1_stage[a, b] = keep.tile([P, PACK, P, PACK], BF16, name=f"w1_stage{a}", align_bytes=64)
+            w1_codes[a, b] = keep.tile([P, KP], U32, name=f"w1_codes{a}{b}", align_bytes=64)
+            w1_sc[a, b] = keep.tile([P, KP], U8, name=f"w1_sc{a}{b}", align_bytes=64)
+
+        def round_w1(copy, a, b, c0, m0, m1):
+            raw = w1_raw[a, b, c0][:, :, PACK * m0 - c0 : PACK * m1 - c0]
+            copy(
+                w1_stage[a, b][:, :, m0:m1, :].rearrange("p t m j -> p m j t"),
+                raw.rearrange("p j (m t) -> p m j t", t=PACK),
+            )
+
+        def quantize_w1(a, b, t0, t1):
+            nc.vector.quantize_mx(
+                out=w1_codes[a, b][:, P * t0 : P * t1].bitcast(FP8X4),
+                scales=w1_sc[a, b][:, P * t0 : P * t1],
+                in_=w1_stage[a, b][:, t0:t1, :, :].rearrange("p t m j -> p (t m j)"),
+            )
+
+        banks = {}
+
+        def stage1_pass(a, b, t):
+            for half in range(2):
+                cols = slice(NB * half, NB * (half + 1))
+                if a == 2:
+                    banks[b, t, half] = psum.tile([P, NB], F32, name=f"bank{2 * t + half}")
+                    c0 = KP * b + P * t
+                    lhsT = w4_codes[:, 2 * c0 : 2 * (c0 + P)].bitcast(FP4X4)
+                    lhsT_scale = w4_sc[:, c0 : c0 + P]
+                else:
+                    lhsT = w1_codes[a, b][:, P * t : P * (t + 1)].bitcast(FP8X4)
+                    lhsT_scale = w1_sc[a, b][:, P * t : P * (t + 1)]
+                nc.tensor.matmul_mx(
+                    out=banks[b, t, half][:],
+                    lhsT=lhsT,
+                    lhsT_scale=lhsT_scale,
+                    rhs=v_words[a][:, cols].bitcast(FP8X4),
+                    rhs_scale=v_scales[SCALE_ROW[a] : P, cols],
+                    start=(a == 2),
+                    stop=(a == 1),
+                )
+
+        feat = {}
+
+        def tanh_plane(b, t):
+            feat[b, t] = hpool.tile([P, S], F32, name="feat")
+            for half in range(2):
+                nc.scalar.activation(feat[b, t][:, NB * half : NB * (half + 1)], banks[b, t, half][:], ACT.Tanh)
+
+        for t in range(PACK):
+            stage1_pass(2, 0, t)
+        gather_tab(0)
+        new_w1(0, 0)
+        round_w1(nc.scalar.copy, 0, 0, 0, 0, P)
+        quantize_w1(0, 0, 0, PACK)
+        for t in range(PACK):
+            stage1_pass(0, 0, t)
+        gather_tab(1)
+        new_w1(1, 0)
+        round_w1(nc.scalar.copy, 1, 0, 0, 0, 64)
+        round_w1(nc.vector.tensor_copy, 1, 0, KP // 2, 64, 112)
+        round_w1(nc.scalar.copy, 1, 0, KP // 2, 112, P)
+        for t in range(PACK):
+            quantize_w1(1, 0, t, t + 1)
+        for t in range(PACK):
+            stage1_pass(1, 0, t)
+            tanh_plane(0, t)
+
+        x1_planes = {}
+        x2_planes = {}
+
+        def gather_x1(b, t, part, parts):
+            n = NP // parts
+            if (b, part) not in x1_planes:
+                tag = (("w1_stage0", "w1_stage1"), ("wide2_1", "stage_b1"))[b][part]
+                x1_planes[b, part] = keep.tile([P, PACK, n], F32, name=f"x1_planes{b}{part}", tag=tag, align_bytes=64)
+            offsets = pos1_sb[:, part * n // 16 : (part + 1) * n // 16]
+            nc.vector.tensor_tensor(
+                x1_planes[b, part][:, t, :], feat[b, t][:].indirect(offsets), wide1[b][:, t, 0:n], ALU.mult
+            )
+
+        y_tiles = {}
+
+        def gather_x2(b, t):
+            y_tiles[b, t] = ring.tile([P, NP], F32, name="y_tile")
+            nc.vector.tensor_tensor(y_tiles[b, t][:], feat[b, t][:].indirect(pos2_sb[:]), wide2[b][:, t, :], ALU.mult)
+
+        def leaky_x2(b, t):
+            if b not in x2_planes:
+                x2_planes[b] = keep.tile([P, PACK, NP], BF16, name=f"x2_planes{b}")
+            y = y_tiles[b, t]
+            nc.vector.scalar_tensor_tensor(
+                x2_planes[b][:, t, :], y[:], slope_sb[:, b, t : t + 1], y[:], ALU.mult, ALU.max
+            )
+
+        x_codes = {}
+        x_sc = {}
+        x_stage = {}
+
+        def weave(copy, key, planes, tag):
+            n = planes.shape[2]
+            x_stage[key] = keep.tile([P, n, PACK], BF16, name="x_stage%s%d%d" % key, tag=tag, align_bytes=64)
+            copy(
+                x_stage[key][:].rearrange("p (c i) t -> p c t i", i=4),
+                planes[:].rearrange("p t (c i) -> p c t i", i=4),
+            )
+
+        def quantize_x(key):
+            n = x_stage[key].shape[1]
+            x_codes[key] = keep.tile([P, n], U32, name="x_codes%s%d%d" % key, align_bytes=64)
+            x_sc[key] = keep.tile([P, n], U8, name="x_sc%s%d%d" % key, align_bytes=64)
+            nc.vector.quantize_mx(
+                out=x_codes[key][:].bitcast(FP8X4),
+                scales=x_sc[key][:],
+                in_=x_stage[key][:].rearrange("p n t -> p (n t)"),
+            )
+
+        for a in range(2):
+            new_w1(a, 1)
+            round_w1(nc.scalar.copy, a, 1, 0, 0, P)
+        for t in range(PACK):
+            gather_x2(0, t)
+            if t > 0:
+                leaky_x2(0, t - 1)
+        quantize_w1(0, 1, 0, PACK)
+        leaky_x2(0, PACK - 1)
+        for t in range(PACK):
+            gather_x1(0, t, 0, 2)
+        quantize_w1(1, 1, 0, PACK)
+        for t in range(PACK):
+            gather_x1(0, t, 1, 2)
+        weave(nc.scalar.copy, ("b", 0, 0), x2_planes[0], "stage_b0")
+        for a in (2, 0, 1):
+            for t in range(PACK):
+                stage1_pass(a, 1, t)
+                if a == 1:
+                    tanh_plane(1, t)
+        quantize_x(("b", 0, 0))
+        weave(nc.scalar.copy, ("a", 0, 0), x1_planes[0, 0], "w1_codes11")
+        weave(nc.scalar.copy, ("a", 0, 1), x1_planes[0, 1], "w1_sc11")
+        for t in range(PACK):
+            gather_x2(1, t)
+            if t > 0:
+                leaky_x2(1, t - 1)
+        gather_x1(1, 0, 0, 2)
+        leaky_x2(1, PACK - 1)
+        weave(nc.scalar.copy, ("b", 1, 0), x2_planes[1], "stage_b1")
+        for t in range(1, PACK):
+            gather_x1(1, t, 0, 2)
+        quantize_x(("a", 0, 0))
+        quantize_x(("a", 0, 1))
+        quantize_x(("b", 1, 0))
+        weave(nc.scalar.copy, ("a", 1, 0), x1_planes[1, 0], "stage_a1")
+        for t in range(PACK):
+            gather_x1(1, t, 1, 2)
+        quantize_x(("a", 1, 0))
+        weave(nc.vector.tensor_copy, ("a", 1, 1), x1_planes[1, 1], "stage_a1")
+        quantize_x(("a", 1, 1))
+
+        scores = [psum.tile([P, NP], F32, name=f"bank{i}") for i in range(NP // P)]
+
+        def stage2_pass(b, i):
+            key, c0 = ("a", b, i // 2), P * (i % 2)
+            nc.tensor.matmul_mx(
+                out=scores[i][:],
+                lhsT=x_codes[key][:, c0 : c0 + P].bitcast(FP8X4),
+                lhsT_scale=x_sc[key][:, c0 : c0 + P],
+                rhs=x_codes["b", b, 0][:].bitcast(FP8X4),
+                rhs_scale=x_sc["b", b, 0][:],
+                start=(b == 0),
+                stop=(b == 1),
+            )
+
+        for i in range(NP // P):
+            stage2_pass(0, i)
+        for i in range(NP // P):
+            stage2_pass(1, i)
+            logits = ring.tile([P, NP], F32, name="logits")
+            nc.vector.tensor_tensor(logits[:], scores[i][:], row_sb[:], ALU.add)
+            prob = ring.tile([P, NP], F32, name="prob")
+            nc.scalar.activation(prob[:], logits[:], ACT.Sigmoid)
+            result = hpool.tile([P, NP], F32, name="result")
+            nc.vector.tensor_scalar(result[:], prob[:], col_sb[:, i : i + 1], None, ALU.mult)
+            nc.sync.dma_start(out=out[P * i : P * (i + 1), :], in_=result[:])

@@ -35,101 +35,94 @@ def tile_list_baton_exchange_scores_kernel(
         hpool = ctx.enter_context(tc.tile_pool(name="hpool", bufs=4))
         psum = ctx.enter_context(tc.psum_pool(name="psum", bufs=1))
 
+        def held(shape, dtype, name, tag=None):
+            return keep.tile(shape, dtype, name=name, tag=tag or name, align_bytes=64)
+
         offs_sb = keep.tile([P, S // 16], U16, name="offs_sb")
         pos1_sb = keep.tile([P, NP // 16], U16, name="pos1_sb")
         pos2_sb = keep.tile([P, NP // 16], U16, name="pos2_sb")
-        tab_sb = [keep.tile([P, T], U32, name=f"tab_sb{a}", align_bytes=64) for a in range(3)]
-        tabsc_sb = keep.tile([P, T], U8, name="tabsc_sb", align_bytes=64)
-        w4_raw = keep.tile([P, 2 * H], U8, name="w4_raw", align_bytes=64)
-        w4sc_raw = keep.tile([P, H], U8, name="w4sc_raw", align_bytes=64)
-        gain_sb = keep.tile([P, 2, PACK], F32, name="gain_sb")
-        slope_sb = keep.tile([P, 2, PACK], F32, name="slope_sb")
-        mix_sb = keep.tile([P, 2, PACK], F32, name="mix_sb")
-        row_sb = keep.tile([P, NP], F32, name="row_sb")
-        col_sb = keep.tile([P, NP // P], F32, name="col_sb")
+        tabsc_sb = held([P, T], U8, "tabsc_sb")
+        w4_raw = held([P, 2 * H], U8, "w4_raw")
+        w4sc_raw = held([P, H], U8, "w4sc_raw")
+        gain_sb = held([P, 2, PACK], F32, "gain_sb")
+        slope_sb = held([P, 2, PACK], F32, "slope_sb")
+        mix_sb = held([P, 2, PACK], F32, "mix_sb")
 
-        def load_tab(a):
+        tab_sb = {}
+
+        def load_tab(a, tag):
+            tab_sb[a] = held([P, T], U32, f"tab_sb{a}", tag)
             nc.sync.dma_start(
                 out=tab_sb[a][:].bitcast(I32), in_=tab_words[a].rearrange("p n t -> p (n t)").bitcast(I32)
             )
 
         w1_raw = {}
 
-        def load_w1(a, b, c0, c1):
-            raw = keep.tile([P, PACK, c1 - c0], F32, name=f"w1_raw{(a + b) % 2}{b * (1 - a)}_{c0}")
+        def load_w1(a, b, c0, c1, tag):
+            raw = held([P, PACK, c1 - c0], F32, f"w1_raw{a}{b}_{c0}", tag)
             w1_raw[a, b, c0] = raw
             rows = w1[KP * a : KP * (a + 1), KP * b + c0 : KP * b + c1]
             nc.sync.dma_start(out=raw[:], in_=rows.rearrange("(p j) c -> p j c", j=PACK))
+
+        def by_channel(vec):
+            return vec.rearrange("(b p t) -> p b t", p=P, t=PACK)
 
         nc.vector.memset(tabsc_sb[:].bitcast(I32), 0)
         nc.vector.memset(w4sc_raw[:].bitcast(I32), 0)
 
         nc.sync.dma_start(offs_sb[:], offs)
-        load_tab(2)
-        for vec_sb, vec in ((gain_sb, gain), (mix_sb, mix), (slope_sb, slope)):
-            nc.scalar.dma_start(out=vec_sb[:], in_=vec.rearrange("(b p t) -> p b t", p=P, t=PACK))
-        nc.sync.dma_start(out=w4_raw[:].bitcast(I32), in_=w4_words[0].bitcast(I32))
-        load_tab(0)
-        load_w1(0, 0, 0, KP)
-        load_tab(1)
+        nc.sync.dma_start(out=gain_sb[:], in_=by_channel(gain))
+        nc.sync.dma_start(out=mix_sb[:], in_=by_channel(mix))
         nc.sync.dma_start(pos1_sb[:], pos1)
         nc.sync.dma_start(pos2_sb[:], pos2)
-        load_w1(1, 0, 0, KP // 2)
-        load_w1(1, 0, KP // 2, KP)
-        load_w1(0, 1, 0, KP)
-        load_w1(1, 1, 0, KP)
-        nc.sync.dma_start(out=row_sb[:], in_=row.partition_broadcast(P))
-        with nc.allow_non_contiguous_dma(reason="one factor for each output row"):
-            nc.sync.dma_start(out=col_sb[:], in_=col.rearrange("(i p) -> p i", p=P))
-
+        nc.sync.dma_start(out=w4_raw[:].bitcast(I32), in_=w4_words[0].bitcast(I32))
+        load_tab(0, "tab_sb0")
+        load_tab(2, "tab_sb2")
         for q in range(4):
-            nc.gpsimd.dma_start(
-                out=tabsc_sb[32 * q : 32 * q + 4, :].bitcast(I32),
-                in_=tab_scales[2, 4 * q : 4 * q + 4, :].bitcast(I32),
-            )
-            nc.gpsimd.dma_start(
+            nc.sync.dma_start(
                 out=tabsc_sb[32 * q + 4 : 32 * q + 12, :].bitcast(I32),
                 in_=tab_scales[0:2, 4 * q : 4 * q + 4, :].bitcast(I32),
+            )
+        for q in range(4):
+            (nc.sync, nc.gpsimd)[q % 2].dma_start(
+                out=tabsc_sb[32 * q : 32 * q + 4, :].bitcast(I32),
+                in_=tab_scales[2, 4 * q : 4 * q + 4, :].bitcast(I32),
             )
         for q in range(4):
             nc.gpsimd.dma_start(
                 out=w4sc_raw[32 * q : 32 * q + 4, :].bitcast(I32),
                 in_=w4_scales[0, 4 * q : 4 * q + 4, :].bitcast(I32),
             )
+        nc.gpsimd.dma_start(out=slope_sb[:], in_=by_channel(slope))
 
-        sign = keep.tile([P, 2, PACK], F32, name="sign")
+        sign = held([P, 2, PACK], F32, "sign")
         fac1 = keep.tile([P, 2, PACK], F32, name="fac1")
-        fac2 = keep.tile([P, 2, PACK], F32, name="fac2")
+        fac2 = held([P, 2, PACK], F32, "fac2")
+        warm = held([P, 1], F32, "warm")
+        nc.scalar.activation(warm[:], gain_sb[:, 0, 0:1], ACT.Sigmoid)
         nc.vector.tensor_scalar(sign[:], mix_sb[:], 0.0, None, ALU.is_ge)
         nc.vector.tensor_scalar(sign[:], sign[:], 2.0, -1.0, ALU.mult, ALU.add)
         nc.vector.tensor_tensor(fac1[:], gain_sb[:], sign[:], ALU.mult)
         nc.vector.tensor_tensor(fac2[:], fac1[:], mix_sb[:], ALU.mult)
+        load_tab(1, "gain_sb")
+        load_w1(0, 0, 0, KP, "mix_sb")
+        load_w1(1, 0, 0, KP // 2, "sign")
         wide1 = [keep.tile([P, PACK, NP], F32, name=f"wide1_{b}") for b in range(2)]
         wide2 = [keep.tile([P, PACK, NP], F32, name=f"wide2_{b}", align_bytes=64) for b in range(2)]
-        for b in range(2):
-            for wide, fac in ((wide2, fac2), (wide1, fac1)):
-                nc.scalar.copy(wide[b][:], fac[:, b, :].unsqueeze(2).to_broadcast([P, PACK, NP]))
 
         v_words = {}
         v_scales = keep.tile([P, S], U8, name="v_scales", align_bytes=64)
 
         def gather_tab(a):
-            tag = ("tabsc_sb", "w4sc_raw", "v_words2")[a]
-            v_words[a] = keep.tile([P, S], U32, name=f"v_words{a}", tag=tag, align_bytes=64)
+            v_words[a] = held([P, S], U32, f"v_words{a}")
             nc.vector.tensor_copy(v_words[a][:], tab_sb[a][:].indirect(offs_sb[:]))
 
         w4_codes = keep.tile([P, 2 * H], U8, name="w4_codes", align_bytes=64)
-        w4_sc = keep.tile([P, H], U8, name="w4_sc", align_bytes=64)
-        gather_tab(2)
         nc.vector.tensor_copy(
-            w4_codes[:].rearrange("p (b t m e) -> p b t m e", b=2, t=PACK, e=2),
-            w4_raw[:].rearrange("p (b m t e) -> p b t m e", b=2, t=PACK, e=2),
+            w4_codes[:].bitcast(U16).rearrange("p (b t m) -> p b t m", b=2, t=PACK),
+            w4_raw[:].bitcast(U16).rearrange("p (b m t) -> p b t m", b=2, t=PACK),
         )
-        nc.vector.tensor_copy(v_scales[:], tabsc_sb[:].indirect(offs_sb[:]))
-        nc.vector.tensor_copy(
-            w4_sc[:].rearrange("p (b t m) -> p b t m", b=2, t=PACK),
-            w4sc_raw[:].rearrange("p (b m t) -> p b t m", b=2, t=PACK),
-        )
+        load_w1(1, 0, KP // 2, KP, "w4_raw")
 
         w1_codes = {}
         w1_sc = {}
@@ -157,10 +150,12 @@ def tile_list_baton_exchange_scores_kernel(
         banks = {}
 
         def stage1_pass(a, b, t):
+            first = 2
             for half in range(2):
                 cols = slice(NB * half, NB * (half + 1))
-                if a == 2:
+                if a == first:
                     banks[b, t, half] = psum.tile([P, NB], F32, name=f"bank{2 * t + half}")
+                if a == 2:
                     c0 = KP * b + P * t
                     lhsT = w4_codes[:, 2 * c0 : 2 * (c0 + P)].bitcast(FP4X4)
                     lhsT_scale = w4_sc[:, c0 : c0 + P]
@@ -173,7 +168,7 @@ def tile_list_baton_exchange_scores_kernel(
                     lhsT_scale=lhsT_scale,
                     rhs=v_words[a][:, cols].bitcast(FP8X4),
                     rhs_scale=v_scales[SCALE_ROW[a] : P, cols],
-                    start=(a == 2),
+                    start=(a == first),
                     stop=(a == 1),
                 )
 
@@ -184,15 +179,28 @@ def tile_list_baton_exchange_scores_kernel(
             for half in range(2):
                 nc.scalar.activation(feat[b, t][:, NB * half : NB * (half + 1)], banks[b, t, half][:], ACT.Tanh)
 
+        gather_tab(0)
+        load_w1(0, 1, 0, KP, "tab_sb0")
+        gather_tab(2)
+        nc.vector.tensor_copy(v_scales[:], tabsc_sb[:].indirect(offs_sb[:]))
+        load_w1(1, 1, 0, KP, "tabsc_sb")
+        w4_sc = held([P, H], U8, "w4_sc", "tab_sb2")
+        nc.vector.tensor_copy(
+            w4_sc[:].rearrange("p (b t m) -> p b t m", b=2, t=PACK),
+            w4sc_raw[:].rearrange("p (b m t) -> p b t m", b=2, t=PACK),
+        )
         for t in range(PACK):
             stage1_pass(2, 0, t)
-        gather_tab(0)
-        new_w1(0, 0)
-        round_w1(nc.scalar.copy, 0, 0, 0, 0, P)
-        quantize_w1(0, 0, 0, PACK)
-        for t in range(PACK):
-            stage1_pass(0, 0, t)
         gather_tab(1)
+        row_sb = held([P, NP], F32, "row_sb", "gain_sb")
+        nc.sync.dma_start(out=row_sb[:], in_=row.partition_broadcast(P))
+        col_sb = held([P, NP // P], F32, "col_sb", "fac2")
+        with nc.allow_non_contiguous_dma(reason="one factor for each output row"):
+            nc.sync.dma_start(out=col_sb[:], in_=col.rearrange("(i p) -> p i", p=P))
+        new_w1(0, 0)
+        round_w1(nc.scalar.copy, 0, 0, 0, 0, 40)
+        round_w1(nc.vector.tensor_copy, 0, 0, 0, 40, P)
+        quantize_w1(0, 0, 0, PACK)
         new_w1(1, 0)
         round_w1(nc.scalar.copy, 1, 0, 0, 0, 64)
         round_w1(nc.vector.tensor_copy, 1, 0, KP // 2, 64, 112)
@@ -200,8 +208,14 @@ def tile_list_baton_exchange_scores_kernel(
         for t in range(PACK):
             quantize_w1(1, 0, t, t + 1)
         for t in range(PACK):
+            stage1_pass(0, 0, t)
             stage1_pass(1, 0, t)
             tanh_plane(0, t)
+        for b in range(2):
+            for wide, fac in ((wide2, fac2), (wide1, fac1)):
+                for t in range(0, PACK, 2):
+                    nc.scalar.copy(wide[b][:, t : t + 2, :], fac[:, b, t : t + 2].unsqueeze(2).to_broadcast([P, 2, NP]))
+
 
         x1_planes = {}
         x2_planes = {}
@@ -234,13 +248,14 @@ def tile_list_baton_exchange_scores_kernel(
         x_sc = {}
         x_stage = {}
 
-        def weave(copy, key, planes, tag):
+        def weave(shares, key, planes, tag):
             n = planes.shape[2]
-            x_stage[key] = keep.tile([P, n, PACK], BF16, name="x_stage%s%d%d" % key, tag=tag, align_bytes=64)
-            copy(
-                x_stage[key][:].rearrange("p (c i) t -> p c t i", i=4),
-                planes[:].rearrange("p t (c i) -> p c t i", i=4),
-            )
+            x_stage[key] = held([P, n, PACK], BF16, "x_stage%s%d%d" % key, tag)
+            for copy, c0, c1 in shares:
+                copy(
+                    x_stage[key][:, c0:c1, :].rearrange("p (c i) t -> p c t i", i=4),
+                    planes[:, :, c0:c1].rearrange("p t (c i) -> p c t i", i=4),
+                )
 
         def quantize_x(key):
             n = x_stage[key].shape[1]
@@ -266,32 +281,32 @@ def tile_list_baton_exchange_scores_kernel(
         quantize_w1(1, 1, 0, PACK)
         for t in range(PACK):
             gather_x1(0, t, 1, 2)
-        weave(nc.scalar.copy, ("b", 0, 0), x2_planes[0], "stage_b0")
+        weave([(nc.scalar.copy, 0, NP)], ("b", 0, 0), x2_planes[0], "stage_b0")
         for a in (2, 0, 1):
             for t in range(PACK):
                 stage1_pass(a, 1, t)
                 if a == 1:
                     tanh_plane(1, t)
         quantize_x(("b", 0, 0))
-        weave(nc.scalar.copy, ("a", 0, 0), x1_planes[0, 0], "w1_codes11")
-        weave(nc.scalar.copy, ("a", 0, 1), x1_planes[0, 1], "w1_sc11")
+        weave([(nc.scalar.copy, 0, NP // 2)], ("a", 0, 0), x1_planes[0, 0], "w1_codes11")
+        weave([(nc.scalar.copy, 0, NP // 2)], ("a", 0, 1), x1_planes[0, 1], "w1_sc11")
         for t in range(PACK):
             gather_x2(1, t)
             if t > 0:
                 leaky_x2(1, t - 1)
         gather_x1(1, 0, 0, 2)
         leaky_x2(1, PACK - 1)
-        weave(nc.scalar.copy, ("b", 1, 0), x2_planes[1], "stage_b1")
+        weave([(nc.scalar.copy, 0, NP)], ("b", 1, 0), x2_planes[1], "stage_b1")
         for t in range(1, PACK):
             gather_x1(1, t, 0, 2)
         quantize_x(("a", 0, 0))
         quantize_x(("a", 0, 1))
         quantize_x(("b", 1, 0))
-        weave(nc.scalar.copy, ("a", 1, 0), x1_planes[1, 0], "stage_a1")
+        weave([(nc.scalar.copy, 0, NP // 2)], ("a", 1, 0), x1_planes[1, 0], "stage_a1")
         for t in range(PACK):
             gather_x1(1, t, 1, 2)
         quantize_x(("a", 1, 0))
-        weave(nc.vector.tensor_copy, ("a", 1, 1), x1_planes[1, 1], "stage_a1")
+        weave([(nc.vector.tensor_copy, 0, 168), (nc.scalar.copy, 168, NP // 2)], ("a", 1, 1), x1_planes[1, 1], "stage_a1")
         quantize_x(("a", 1, 1))
 
         scores = [psum.tile([P, NP], F32, name=f"bank{i}") for i in range(NP // P)]
@@ -312,10 +327,13 @@ def tile_list_baton_exchange_scores_kernel(
             stage2_pass(0, i)
         for i in range(NP // P):
             stage2_pass(1, i)
-            logits = ring.tile([P, NP], F32, name="logits")
+            logits = hpool.tile([P, NP], F32, name="logits")
             nc.vector.tensor_tensor(logits[:], scores[i][:], row_sb[:], ALU.add)
-            prob = ring.tile([P, NP], F32, name="prob")
+            prob = hpool.tile([P, NP], F32, name="prob")
             nc.scalar.activation(prob[:], logits[:], ACT.Sigmoid)
             result = hpool.tile([P, NP], F32, name="result")
-            nc.vector.tensor_scalar(result[:], prob[:], col_sb[:, i : i + 1], None, ALU.mult)
+            if i < 2:
+                nc.gpsimd.tensor_scalar(result[:], prob[:], col_sb[:, i : i + 1], 0.0, ALU.mult, ALU.add)
+            else:
+                nc.vector.tensor_scalar(result[:], prob[:], col_sb[:, i : i + 1], None, ALU.mult)
             nc.sync.dma_start(out=out[P * i : P * (i + 1), :], in_=result[:])

@@ -31,7 +31,6 @@ def tile_list_baton_exchange_scores_kernel(
     nc = tc.nc
     with ExitStack() as ctx:
         keep = ctx.enter_context(tc.tile_pool(name="keep", bufs=1))
-        ring = ctx.enter_context(tc.tile_pool(name="ring", bufs=2))
         hpool = ctx.enter_context(tc.tile_pool(name="hpool", bufs=4))
         psum = ctx.enter_context(tc.psum_pool(name="psum", bufs=1))
 
@@ -71,32 +70,29 @@ def tile_list_baton_exchange_scores_kernel(
         nc.vector.memset(w4sc_raw[:].bitcast(I32), 0)
 
         nc.sync.dma_start(offs_sb[:], offs)
-        nc.sync.dma_start(out=gain_sb[:], in_=by_channel(gain))
-        nc.sync.dma_start(out=mix_sb[:], in_=by_channel(mix))
+        load_tab(0, "tab_sb0")
+        for vec_sb, vec in ((gain_sb, gain), (mix_sb, mix), (slope_sb, slope)):
+            nc.scalar.dma_start(out=vec_sb[:], in_=by_channel(vec))
+        nc.sync.dma_start(out=w4_raw[:].bitcast(I32), in_=w4_words[0].bitcast(I32))
+        load_tab(2, "tab_sb2")
+        load_tab(1, "tab_sb1")
         nc.sync.dma_start(pos1_sb[:], pos1)
         nc.sync.dma_start(pos2_sb[:], pos2)
-        nc.sync.dma_start(out=w4_raw[:].bitcast(I32), in_=w4_words[0].bitcast(I32))
-        load_tab(0, "tab_sb0")
-        load_tab(2, "tab_sb2")
+        load_w1(0, 0, 0, KP, "w1_raw00")
+        load_w1(1, 0, 0, KP // 2, "w1_raw10_lo")
+        load_w1(1, 0, KP // 2, KP, "w1_raw10_hi")
         for q in range(4):
-            nc.sync.dma_start(
+            nc.gpsimd.dma_start(
                 out=tabsc_sb[32 * q + 4 : 32 * q + 12, :].bitcast(I32),
                 in_=tab_scales[0:2, 4 * q : 4 * q + 4, :].bitcast(I32),
             )
-        for q in range(4):
-            (nc.sync, nc.gpsimd)[q % 2].dma_start(
-                out=tabsc_sb[32 * q : 32 * q + 4, :].bitcast(I32),
-                in_=tab_scales[2, 4 * q : 4 * q + 4, :].bitcast(I32),
-            )
-        for q in range(4):
-            nc.gpsimd.dma_start(
-                out=w4sc_raw[32 * q : 32 * q + 4, :].bitcast(I32),
-                in_=w4_scales[0, 4 * q : 4 * q + 4, :].bitcast(I32),
-            )
-        nc.gpsimd.dma_start(out=slope_sb[:], in_=by_channel(slope))
+        for r in range(4):
+            nc.gpsimd.dma_start(out=tabsc_sb[r:P:32, :].bitcast(I32), in_=tab_scales[2, r:16:4, :].bitcast(I32))
+        for r in range(4):
+            nc.gpsimd.dma_start(out=w4sc_raw[r:P:32, :].bitcast(I32), in_=w4_scales[0, r:16:4, :].bitcast(I32))
 
         sign = held([P, 2, PACK], F32, "sign")
-        fac1 = keep.tile([P, 2, PACK], F32, name="fac1")
+        fac1 = held([P, 2, PACK], F32, "fac1")
         fac2 = held([P, 2, PACK], F32, "fac2")
         warm = held([P, 1], F32, "warm")
         nc.scalar.activation(warm[:], gain_sb[:, 0, 0:1], ACT.Sigmoid)
@@ -104,11 +100,9 @@ def tile_list_baton_exchange_scores_kernel(
         nc.vector.tensor_scalar(sign[:], sign[:], 2.0, -1.0, ALU.mult, ALU.add)
         nc.vector.tensor_tensor(fac1[:], gain_sb[:], sign[:], ALU.mult)
         nc.vector.tensor_tensor(fac2[:], fac1[:], mix_sb[:], ALU.mult)
-        load_tab(1, "gain_sb")
-        load_w1(0, 0, 0, KP, "mix_sb")
-        load_w1(1, 0, 0, KP // 2, "sign")
-        wide1 = [keep.tile([P, PACK, NP], F32, name=f"wide1_{b}") for b in range(2)]
-        wide2 = [keep.tile([P, PACK, NP], F32, name=f"wide2_{b}", align_bytes=64) for b in range(2)]
+
+        wide1 = [held([P, PACK, NP // 2], F32, f"wide1_{b}") for b in range(2)]
+        wide2 = {(b, t): held([P, NP], F32, f"wide2_{b}{t}") for b in range(2) for t in range(PACK)}
 
         v_words = {}
         v_scales = keep.tile([P, S], U8, name="v_scales", align_bytes=64)
@@ -122,7 +116,6 @@ def tile_list_baton_exchange_scores_kernel(
             w4_codes[:].bitcast(U16).rearrange("p (b t m) -> p b t m", b=2, t=PACK),
             w4_raw[:].bitcast(U16).rearrange("p (b m t) -> p b t m", b=2, t=PACK),
         )
-        load_w1(1, 0, KP // 2, KP, "w4_raw")
 
         w1_codes = {}
         w1_sc = {}
@@ -136,8 +129,8 @@ def tile_list_baton_exchange_scores_kernel(
         def round_w1(copy, a, b, c0, m0, m1):
             raw = w1_raw[a, b, c0][:, :, PACK * m0 - c0 : PACK * m1 - c0]
             copy(
-                w1_stage[a, b][:, :, m0:m1, :].rearrange("p t m j -> p m j t"),
-                raw.rearrange("p j (m t) -> p m j t", t=PACK),
+                w1_stage[a, b][:, :, m0:m1, :].rearrange("p t m j -> p m t j"),
+                raw.rearrange("p j (m t) -> p m t j", t=PACK),
             )
 
         def quantize_w1(a, b, t0, t1):
@@ -192,9 +185,9 @@ def tile_list_baton_exchange_scores_kernel(
         for t in range(PACK):
             stage1_pass(2, 0, t)
         gather_tab(1)
-        row_sb = held([P, NP], F32, "row_sb", "gain_sb")
+        row_sb = held([P, NP], F32, "row_sb", "tab_sb1")
         nc.sync.dma_start(out=row_sb[:], in_=row.partition_broadcast(P))
-        col_sb = held([P, NP // P], F32, "col_sb", "fac2")
+        col_sb = held([P, NP // P], F32, "col_sb", "w4sc_raw")
         with nc.allow_non_contiguous_dma(reason="one factor for each output row"):
             nc.sync.dma_start(out=col_sb[:], in_=col.rearrange("(i p) -> p i", p=P))
         new_w1(0, 0)
@@ -212,10 +205,9 @@ def tile_list_baton_exchange_scores_kernel(
             stage1_pass(1, 0, t)
             tanh_plane(0, t)
         for b in range(2):
-            for wide, fac in ((wide2, fac2), (wide1, fac1)):
-                for t in range(0, PACK, 2):
-                    nc.scalar.copy(wide[b][:, t : t + 2, :], fac[:, b, t : t + 2].unsqueeze(2).to_broadcast([P, 2, NP]))
-
+            for t in range(PACK):
+                nc.scalar.copy(wide2[b, t][:], fac2[:, b, t : t + 1].to_broadcast([P, NP]))
+            nc.scalar.copy(wide1[b][:], fac1[:, b, :].unsqueeze(2).to_broadcast([P, PACK, NP // 2]))
 
         x1_planes = {}
         x2_planes = {}
@@ -223,22 +215,22 @@ def tile_list_baton_exchange_scores_kernel(
         def gather_x1(b, t, part, parts):
             n = NP // parts
             if (b, part) not in x1_planes:
-                tag = (("w1_stage0", "w1_stage1"), ("wide2_1", "stage_b1"))[b][part]
+                tag = (("x1_planes00", "w1_stage1"), ("wide2_13", "stage_b1"))[b][part]
                 x1_planes[b, part] = keep.tile([P, PACK, n], F32, name=f"x1_planes{b}{part}", tag=tag, align_bytes=64)
             offsets = pos1_sb[:, part * n // 16 : (part + 1) * n // 16]
             nc.vector.tensor_tensor(
-                x1_planes[b, part][:, t, :], feat[b, t][:].indirect(offsets), wide1[b][:, t, 0:n], ALU.mult
+                x1_planes[b, part][:, t, :], feat[b, t][:].indirect(offsets), wide1[b][:, t, :], ALU.mult
             )
 
         y_tiles = {}
 
         def gather_x2(b, t):
-            y_tiles[b, t] = ring.tile([P, NP], F32, name="y_tile")
-            nc.vector.tensor_tensor(y_tiles[b, t][:], feat[b, t][:].indirect(pos2_sb[:]), wide2[b][:, t, :], ALU.mult)
+            y_tiles[b, t] = held([P, NP], F32, f"y_tile{b}{t}", "w1_stage0" if (b, t) == (0, 3) else f"y_tile{t}")
+            nc.vector.tensor_tensor(y_tiles[b, t][:], feat[b, t][:].indirect(pos2_sb[:]), wide2[b, t][:], ALU.mult)
 
         def leaky_x2(b, t):
             if b not in x2_planes:
-                x2_planes[b] = keep.tile([P, PACK, NP], BF16, name=f"x2_planes{b}")
+                x2_planes[b] = held([P, PACK, NP], BF16, f"x2_planes{b}", ("x2_planes0", "wide2_12")[b])
             y = y_tiles[b, t]
             nc.vector.scalar_tensor_tensor(
                 x2_planes[b][:, t, :], y[:], slope_sb[:, b, t : t + 1], y[:], ALU.mult, ALU.max
@@ -253,8 +245,8 @@ def tile_list_baton_exchange_scores_kernel(
             x_stage[key] = held([P, n, PACK], BF16, "x_stage%s%d%d" % key, tag)
             for copy, c0, c1 in shares:
                 copy(
-                    x_stage[key][:, c0:c1, :].rearrange("p (c i) t -> p c t i", i=4),
-                    planes[:, :, c0:c1].rearrange("p t (c i) -> p c t i", i=4),
+                    x_stage[key][:, c0:c1, :].rearrange("p (c i) t -> p c t i", i=2),
+                    planes[:, :, c0:c1].rearrange("p t (c i) -> p c t i", i=2),
                 )
 
         def quantize_x(key):
@@ -271,13 +263,11 @@ def tile_list_baton_exchange_scores_kernel(
             new_w1(a, 1)
             round_w1(nc.scalar.copy, a, 1, 0, 0, P)
         for t in range(PACK):
+            if t == PACK - 1:
+                quantize_w1(0, 1, 0, PACK)
             gather_x2(0, t)
-            if t > 0:
-                leaky_x2(0, t - 1)
-        quantize_w1(0, 1, 0, PACK)
-        leaky_x2(0, PACK - 1)
-        for t in range(PACK):
             gather_x1(0, t, 0, 2)
+            leaky_x2(0, t)
         quantize_w1(1, 1, 0, PACK)
         for t in range(PACK):
             gather_x1(0, t, 1, 2)
@@ -290,10 +280,11 @@ def tile_list_baton_exchange_scores_kernel(
         quantize_x(("b", 0, 0))
         weave([(nc.scalar.copy, 0, NP // 2)], ("a", 0, 0), x1_planes[0, 0], "w1_codes11")
         weave([(nc.scalar.copy, 0, NP // 2)], ("a", 0, 1), x1_planes[0, 1], "w1_sc11")
-        for t in range(PACK):
+        for t in range(PACK - 1):
             gather_x2(1, t)
-            if t > 0:
-                leaky_x2(1, t - 1)
+        for t in range(PACK - 1):
+            leaky_x2(1, t)
+        gather_x2(1, PACK - 1)
         gather_x1(1, 0, 0, 2)
         leaky_x2(1, PACK - 1)
         weave([(nc.scalar.copy, 0, NP)], ("b", 1, 0), x2_planes[1], "stage_b1")

@@ -74,11 +74,11 @@ def tile_list_baton_exchange_scores_kernel(
         for vec_sb, vec in ((gain_sb, gain), (mix_sb, mix), (slope_sb, slope)):
             nc.scalar.dma_start(out=vec_sb[:], in_=by_channel(vec))
         nc.sync.dma_start(out=w4_raw[:].bitcast(I32), in_=w4_words[0].bitcast(I32))
+        load_w1(0, 0, 0, KP, "w1_raw00")
         load_tab(2, "tab_sb2")
         load_tab(1, "tab_sb1")
         nc.sync.dma_start(pos1_sb[:], pos1)
         nc.sync.dma_start(pos2_sb[:], pos2)
-        load_w1(0, 0, 0, KP, "w1_raw00")
         load_w1(1, 0, 0, KP // 2, "w1_raw10_lo")
         load_w1(1, 0, KP // 2, KP, "w1_raw10_hi")
         for q in range(4):
@@ -143,7 +143,7 @@ def tile_list_baton_exchange_scores_kernel(
         banks = {}
 
         def stage1_pass(a, b, t):
-            first = 2
+            first = (0, 2)[b]
             for half in range(2):
                 cols = slice(NB * half, NB * (half + 1))
                 if a == first:
@@ -174,9 +174,14 @@ def tile_list_baton_exchange_scores_kernel(
 
         gather_tab(0)
         load_w1(0, 1, 0, KP, "tab_sb0")
-        gather_tab(2)
         nc.vector.tensor_copy(v_scales[:], tabsc_sb[:].indirect(offs_sb[:]))
         load_w1(1, 1, 0, KP, "tabsc_sb")
+        new_w1(0, 0)
+        round_w1(nc.scalar.copy, 0, 0, 0, 0, P)
+        quantize_w1(0, 0, 0, PACK)
+        for t in range(PACK):
+            stage1_pass(0, 0, t)
+        gather_tab(2)
         w4_sc = held([P, H], U8, "w4_sc", "tab_sb2")
         nc.vector.tensor_copy(
             w4_sc[:].rearrange("p (b t m) -> p b t m", b=2, t=PACK),
@@ -190,10 +195,6 @@ def tile_list_baton_exchange_scores_kernel(
         col_sb = held([P, NP // P], F32, "col_sb", "w4sc_raw")
         with nc.allow_non_contiguous_dma(reason="one factor for each output row"):
             nc.sync.dma_start(out=col_sb[:], in_=col.rearrange("(i p) -> p i", p=P))
-        new_w1(0, 0)
-        round_w1(nc.scalar.copy, 0, 0, 0, 0, 40)
-        round_w1(nc.vector.tensor_copy, 0, 0, 0, 40, P)
-        quantize_w1(0, 0, 0, PACK)
         new_w1(1, 0)
         round_w1(nc.scalar.copy, 1, 0, 0, 0, 64)
         round_w1(nc.vector.tensor_copy, 1, 0, KP // 2, 64, 112)
@@ -201,7 +202,6 @@ def tile_list_baton_exchange_scores_kernel(
         for t in range(PACK):
             quantize_w1(1, 0, t, t + 1)
         for t in range(PACK):
-            stage1_pass(0, 0, t)
             stage1_pass(1, 0, t)
             tanh_plane(0, t)
         for b in range(2):
@@ -271,14 +271,13 @@ def tile_list_baton_exchange_scores_kernel(
         quantize_w1(1, 1, 0, PACK)
         for t in range(PACK):
             gather_x1(0, t, 1, 2)
-        weave([(nc.scalar.copy, 0, NP)], ("b", 0, 0), x2_planes[0], "stage_b0")
         for a in (2, 0, 1):
             for t in range(PACK):
                 stage1_pass(a, 1, t)
                 if a == 1:
                     tanh_plane(1, t)
-        quantize_x(("b", 0, 0))
-        weave([(nc.scalar.copy, 0, NP // 2)], ("a", 0, 0), x1_planes[0, 0], "w1_codes11")
+        weave([(nc.scalar.copy, 0, NP // 2)], ("a", 0, 0), x1_planes[0, 0], "stage_a0")
+        weave([(nc.scalar.copy, 0, NP)], ("b", 0, 0), x2_planes[0], "w1_codes11")
         weave([(nc.scalar.copy, 0, NP // 2)], ("a", 0, 1), x1_planes[0, 1], "w1_sc11")
         for t in range(PACK - 1):
             gather_x2(1, t)
@@ -291,6 +290,7 @@ def tile_list_baton_exchange_scores_kernel(
         for t in range(1, PACK):
             gather_x1(1, t, 0, 2)
         quantize_x(("a", 0, 0))
+        quantize_x(("b", 0, 0))
         quantize_x(("a", 0, 1))
         quantize_x(("b", 1, 0))
         weave([(nc.scalar.copy, 0, NP // 2)], ("a", 1, 0), x1_planes[1, 0], "stage_a1")
@@ -323,8 +323,5 @@ def tile_list_baton_exchange_scores_kernel(
             prob = hpool.tile([P, NP], F32, name="prob")
             nc.scalar.activation(prob[:], logits[:], ACT.Sigmoid)
             result = hpool.tile([P, NP], F32, name="result")
-            if i < 2:
-                nc.gpsimd.tensor_scalar(result[:], prob[:], col_sb[:, i : i + 1], 0.0, ALU.mult, ALU.add)
-            else:
-                nc.vector.tensor_scalar(result[:], prob[:], col_sb[:, i : i + 1], None, ALU.mult)
+            nc.vector.tensor_scalar(result[:], prob[:], col_sb[:, i : i + 1], None, ALU.mult)
             nc.sync.dma_start(out=out[P * i : P * (i + 1), :], in_=result[:])

@@ -31,7 +31,7 @@ def tile_list_baton_exchange_scores_kernel(
     nc = tc.nc
     with ExitStack() as ctx:
         keep = ctx.enter_context(tc.tile_pool(name="keep", bufs=1))
-        hpool = ctx.enter_context(tc.tile_pool(name="hpool", bufs=4))
+        hpool = ctx.enter_context(tc.tile_pool(name="hpool", bufs=5))
         psum = ctx.enter_context(tc.psum_pool(name="psum", bufs=1))
 
         def held(shape, dtype, name, tag=None):
@@ -77,10 +77,10 @@ def tile_list_baton_exchange_scores_kernel(
         load_w1(0, 0, 0, KP, "w1_raw00")
         load_tab(2, "tab_sb2")
         load_tab(1, "tab_sb1")
-        nc.sync.dma_start(pos1_sb[:], pos1)
-        nc.sync.dma_start(pos2_sb[:], pos2)
         load_w1(1, 0, 0, KP // 2, "w1_raw10_lo")
         load_w1(1, 0, KP // 2, KP, "w1_raw10_hi")
+        nc.sync.dma_start(pos2_sb[:], pos2)
+        nc.sync.dma_start(pos1_sb[:], pos1)
         for q in range(4):
             nc.gpsimd.dma_start(
                 out=tabsc_sb[32 * q + 4 : 32 * q + 12, :].bitcast(I32),
@@ -126,11 +126,11 @@ def tile_list_baton_exchange_scores_kernel(
             w1_codes[a, b] = keep.tile([P, KP], U32, name=f"w1_codes{a}{b}", align_bytes=64)
             w1_sc[a, b] = keep.tile([P, KP], U8, name=f"w1_sc{a}{b}", align_bytes=64)
 
-        def round_w1(copy, a, b, c0, m0, m1):
+        def round_w1(copy, a, b, c0, m0, m1, t0=0, t1=PACK):
             raw = w1_raw[a, b, c0][:, :, PACK * m0 - c0 : PACK * m1 - c0]
             copy(
-                w1_stage[a, b][:, :, m0:m1, :].rearrange("p t m j -> p m t j"),
-                raw.rearrange("p j (m t) -> p m t j", t=PACK),
+                w1_stage[a, b][:, t0:t1, m0:m1, :].rearrange("p t m j -> p m t j"),
+                raw.rearrange("p j (m t) -> p m t j", t=PACK)[:, :, t0:t1, :],
             )
 
         def quantize_w1(a, b, t0, t1):
@@ -197,10 +197,10 @@ def tile_list_baton_exchange_scores_kernel(
             nc.sync.dma_start(out=col_sb[:], in_=col.rearrange("(i p) -> p i", p=P))
         new_w1(1, 0)
         round_w1(nc.scalar.copy, 1, 0, 0, 0, 64)
-        round_w1(nc.vector.tensor_copy, 1, 0, KP // 2, 64, 112)
-        round_w1(nc.scalar.copy, 1, 0, KP // 2, 112, P)
-        for t in range(PACK):
-            quantize_w1(1, 0, t, t + 1)
+        round_w1(nc.vector.tensor_copy, 1, 0, KP // 2, 64, P, 0, 1)
+        quantize_w1(1, 0, 0, 1)
+        round_w1(nc.vector.tensor_copy, 1, 0, KP // 2, 64, P, 1, PACK)
+        quantize_w1(1, 0, 1, PACK)
         for t in range(PACK):
             stage1_pass(1, 0, t)
             tanh_plane(0, t)
@@ -212,14 +212,12 @@ def tile_list_baton_exchange_scores_kernel(
         x1_planes = {}
         x2_planes = {}
 
-        def gather_x1(b, t, part, parts):
-            n = NP // parts
-            if (b, part) not in x1_planes:
-                tag = (("x1_planes00", "w1_stage1"), ("wide2_13", "stage_b1"))[b][part]
-                x1_planes[b, part] = keep.tile([P, PACK, n], F32, name=f"x1_planes{b}{part}", tag=tag, align_bytes=64)
-            offsets = pos1_sb[:, part * n // 16 : (part + 1) * n // 16]
+        def gather_x1(b, t, m0, n, tag):
+            if t == 0:
+                x1_planes[b, m0] = held([P, PACK, n], F32, f"x1_planes{b}_{m0}", tag)
+            offsets = pos1_sb[:, m0 // 16 : (m0 + n) // 16]
             nc.vector.tensor_tensor(
-                x1_planes[b, part][:, t, :], feat[b, t][:].indirect(offsets), wide1[b][:, t, :], ALU.mult
+                x1_planes[b, m0][:, t, :], feat[b, t][:].indirect(offsets), wide1[b][:, t, 0:n], ALU.mult
             )
 
         y_tiles = {}
@@ -266,11 +264,11 @@ def tile_list_baton_exchange_scores_kernel(
             if t == PACK - 1:
                 quantize_w1(0, 1, 0, PACK)
             gather_x2(0, t)
-            gather_x1(0, t, 0, 2)
+            gather_x1(0, t, 0, 256, None)
             leaky_x2(0, t)
         quantize_w1(1, 1, 0, PACK)
         for t in range(PACK):
-            gather_x1(0, t, 1, 2)
+            gather_x1(0, t, 256, 256, "w1_stage1")
         for a in (2, 0, 1):
             for t in range(PACK):
                 stage1_pass(a, 1, t)
@@ -278,32 +276,35 @@ def tile_list_baton_exchange_scores_kernel(
                     tanh_plane(1, t)
         weave([(nc.scalar.copy, 0, NP // 2)], ("a", 0, 0), x1_planes[0, 0], "stage_a0")
         weave([(nc.scalar.copy, 0, NP)], ("b", 0, 0), x2_planes[0], "w1_codes11")
-        weave([(nc.scalar.copy, 0, NP // 2)], ("a", 0, 1), x1_planes[0, 1], "w1_sc11")
+        weave([(nc.scalar.copy, 0, NP // 2)], ("a", 0, 1), x1_planes[0, 256], "w1_sc11")
         for t in range(PACK - 1):
             gather_x2(1, t)
         for t in range(PACK - 1):
             leaky_x2(1, t)
         gather_x2(1, PACK - 1)
-        gather_x1(1, 0, 0, 2)
+        gather_x1(1, 0, 0, 256, "wide2_13")
         leaky_x2(1, PACK - 1)
         weave([(nc.scalar.copy, 0, NP)], ("b", 1, 0), x2_planes[1], "stage_b1")
         for t in range(1, PACK):
-            gather_x1(1, t, 0, 2)
+            gather_x1(1, t, 0, 256, None)
         quantize_x(("a", 0, 0))
         quantize_x(("b", 0, 0))
         quantize_x(("a", 0, 1))
         quantize_x(("b", 1, 0))
         weave([(nc.scalar.copy, 0, NP // 2)], ("a", 1, 0), x1_planes[1, 0], "stage_a1")
         for t in range(PACK):
-            gather_x1(1, t, 1, 2)
+            gather_x1(1, t, 256, P, "stage_b1")
         quantize_x(("a", 1, 0))
-        weave([(nc.vector.tensor_copy, 0, 168), (nc.scalar.copy, 168, NP // 2)], ("a", 1, 1), x1_planes[1, 1], "stage_a1")
-        quantize_x(("a", 1, 1))
+        weave([(nc.scalar.copy, 0, P)], ("a", 1, 2), x1_planes[1, 256], None)
+        for t in range(PACK):
+            gather_x1(1, t, 384, P, "stage_a1")
+        quantize_x(("a", 1, 2))
+        weave([(nc.vector.tensor_copy, 0, P)], ("a", 1, 3), x1_planes[1, 384], None)
 
         scores = [psum.tile([P, NP], F32, name=f"bank{i}") for i in range(NP // P)]
 
         def stage2_pass(b, i):
-            key, c0 = ("a", b, i // 2), P * (i % 2)
+            key, c0 = (("a", b, i // 2), P * (i % 2)) if b == 0 or i < 2 else (("a", b, i), 0)
             nc.tensor.matmul_mx(
                 out=scores[i][:],
                 lhsT=x_codes[key][:, c0 : c0 + P].bitcast(FP8X4),
@@ -314,14 +315,26 @@ def tile_list_baton_exchange_scores_kernel(
                 stop=(b == 1),
             )
 
+        def finish(i, j0, j1):
+            logits = hpool.tile([P, j1 - j0], F32, name="logits")
+            nc.vector.tensor_tensor(logits[:], scores[i][:, j0:j1], row_sb[:, j0:j1], ALU.add)
+            prob = hpool.tile([P, j1 - j0], F32, name="prob")
+            nc.scalar.activation(prob[:], logits[:], ACT.Sigmoid)
+            result = hpool.tile([P, j1 - j0], F32, name="result")
+            if i == 0:
+                nc.scalar.activation(result[:], prob[:], ACT.Copy, scale=col_sb[:, i : i + 1])
+            else:
+                nc.vector.tensor_scalar(result[:], prob[:], col_sb[:, i : i + 1], None, ALU.mult)
+            nc.sync.dma_start(out=out[P * i : P * (i + 1), j0:j1], in_=result[:])
+
         for i in range(NP // P):
             stage2_pass(0, i)
-        for i in range(NP // P):
+        for i in range(NP // P - 1):
             stage2_pass(1, i)
-            logits = hpool.tile([P, NP], F32, name="logits")
-            nc.vector.tensor_tensor(logits[:], scores[i][:], row_sb[:], ALU.add)
-            prob = hpool.tile([P, NP], F32, name="prob")
-            nc.scalar.activation(prob[:], logits[:], ACT.Sigmoid)
-            result = hpool.tile([P, NP], F32, name="result")
-            nc.vector.tensor_scalar(result[:], prob[:], col_sb[:, i : i + 1], None, ALU.mult)
-            nc.sync.dma_start(out=out[P * i : P * (i + 1), :], in_=result[:])
+        finish(0, 0, NP)
+        quantize_x(("a", 1, 3))
+        stage2_pass(1, 3)
+        finish(1, 0, NP)
+        finish(2, 0, NP)
+        finish(3, 0, NP // 2)
+        finish(3, NP // 2, NP)

from contextlib import ExitStack

import concourse.mybir as mybir

F32 = mybir.dt.float32
BF16 = mybir.dt.bfloat16
I32 = mybir.dt.int32
U32 = mybir.dt.uint32
U16 = mybir.dt.uint16
U8 = mybir.dt.uint8
FP8X4 = mybir.dt.float8_e4m3fn_x4
FP4X4 = mybir.dt.float4_e2m1fn_x4
ALU = mybir.AluOpType
ACT = mybir.ActivationFunctionType

P = 128
PACK = 4
KP = 512
T = 4096
S = 1024
H = 1024
NP = 512
NB = 512
FLOPS = 2 * 1536 * H * S + 2 * H * NP * NP
SCALE_ROW = (4, 8, 0)


def tile_list_baton_exchange_scores_kernel(
    tc, tab_words, tab_scales, offs, pos1, pos2, w1, w4_words, w4_scales, gain, slope, mix, row, col, out
):
    nc = tc.nc
    with ExitStack() as ctx:
        keep = ctx.enter_context(tc.tile_pool(name="keep", bufs=1))
        hpool = ctx.enter_context(tc.tile_pool(name="hpool", bufs=5))
        psum = ctx.enter_context(tc.psum_pool(name="psum", bufs=1))

        def held(shape, dtype, name, tag=None):
            return keep.tile(shape, dtype, name=name, tag=tag or name, align_bytes=64)

        offs_sb = keep.tile([P, S // 16], U16, name="offs_sb")
        pos1_sb = keep.tile([P, NP // 16], U16, name="pos1_sb")
        pos2_sb = keep.tile([P, NP // 16], U16, name="pos2_sb")
        tabsc_sb = held([P, T], U8, "tabsc_sb")
        w4_raw = held([P, 2 * H], U8, "w4_raw")
        w4sc_raw = held([P, H], U8, "w4sc_raw")
        gain_sb = held([P, 2, PACK], F32, "gain_sb")
        slope_sb = held([P, 2, PACK], F32, "slope_sb")
        mix_sb = held([P, 2, PACK], F32, "mix_sb")

        tab_sb = {}

        def load_tab(a, tag):
            tab_sb[a] = held([P, T], U32, f"tab_sb{a}", tag)
            nc.sync.dma_start(
                out=tab_sb[a][:].bitcast(I32), in_=tab_words[a].rearrange("p n t -> p (n t)").bitcast(I32)
            )

        w1_raw = {}

        def load_w1(a, b, c0, c1, tag):
            raw = held([P, PACK, c1 - c0], F32, f"w1_raw{a}{b}_{c0}", tag)
            w1_raw[a, b, c0] = raw
            rows = w1[KP * a : KP * (a + 1), KP * b + c0 : KP * b + c1]
            nc.sync.dma_start(out=raw[:], in_=rows.rearrange("(p j) c -> p j c", j=PACK))

        def by_channel(vec):
            return vec.rearrange("(b p t) -> p b t", p=P, t=PACK)

        nc.vector.memset(tabsc_sb[:].bitcast(I32), 0)
        nc.vector.memset(w4sc_raw[:].bitcast(I32), 0)

        nc.sync.dma_start(offs_sb[:], offs)
        load_tab(0, "tab_sb0")
        for vec_sb, vec in ((gain_sb, gain), (mix_sb, mix), (slope_sb, slope)):
            nc.scalar.dma_start(out=vec_sb[:], in_=by_channel(vec))
        nc.sync.dma_start(out=w4_raw[:].bitcast(I32), in_=w4_words[0].bitcast(I32))
        load_w1(0, 0, 0, KP, "w1_raw00")
        load_tab(2, "tab_sb2")
        load_tab(1, "tab_sb1")
        load_w1(1, 0, 0, KP // 2, "w1_raw10_lo")
        load_w1(1, 0, KP // 2, KP, "w1_raw10_hi")
        nc.sync.dma_start(pos2_sb[:], pos2)
        nc.sync.dma_start(pos1_sb[:], pos1)
        for q in range(4):
            nc.gpsimd.dma_start(
                out=tabsc_sb[32 * q + 4 : 32 * q + 12, :].bitcast(I32),
                in_=tab_scales[0:2, 4 * q : 4 * q + 4, :].bitcast(I32),
            )
        for r in range(4):
            nc.gpsimd.dma_start(out=tabsc_sb[r:P:32, :].bitcast(I32), in_=tab_scales[2, r:16:4, :].bitcast(I32))
        for r in range(4):
            nc.gpsimd.dma_start(out=w4sc_raw[r:P:32, :].bitcast(I32), in_=w4_scales[0, r:16:4, :].bitcast(I32))

        sign = held([P, 2, PACK], F32, "sign")
        fac1 = held([P, 2, PACK], F32, "fac1")
        fac2 = held([P, 2, PACK], F32, "fac2")
        warm = held([P, 1], F32, "warm")
        nc.scalar.activation(warm[:], gain_sb[:, 0, 0:1], ACT.Sigmoid)
        nc.vector.tensor_scalar(sign[:], mix_sb[:], 0.0, None, ALU.is_ge)
        nc.vector.tensor_scalar(sign[:], sign[:], 2.0, -1.0, ALU.mult, ALU.add)
        nc.vector.tensor_tensor(fac1[:], gain_sb[:], sign[:], ALU.mult)
        nc.vector.tensor_tensor(fac2[:], fac1[:], mix_sb[:], ALU.mult)

        wide1 = [held([P, PACK, NP // 2], F32, f"wide1_{b}") for b in range(2)]
        wide2 = {(b, t): held([P, NP], F32, f"wide2_{b}{t}") for b in range(2) for t in range(PACK)}

        v_words = {}
        v_scales = keep.tile([P, S], U8, name="v_scales", align_bytes=64)

        def gather_tab(a):
            v_words[a] = held([P, S], U32, f"v_words{a}")
            nc.vector.tensor_copy(v_words[a][:], tab_sb[a][:].indirect(offs_sb[:]))

        w4_codes = keep.tile([P, 2 * H], U8, name="w4_codes", align_bytes=64)
        nc.vector.tensor_copy(
            w4_codes[:].bitcast(U16).rearrange("p (b t m) -> p b t m", b=2, t=PACK),
            w4_raw[:].bitcast(U16).rearrange("p (b m t) -> p b t m", b=2, t=PACK),
        )

        w1_codes = {}
        w1_sc = {}
        w1_stage = {}

        def new_w1(a, b):
            w1_stage[a, b] = keep.tile([P, PACK, P, PACK], BF16, name=f"w1_stage{a}", align_bytes=64)
            w1_codes[a, b] = keep.tile([P, KP], U32, name=f"w1_codes{a}{b}", align_bytes=64)
            w1_sc[a, b] = keep.tile([P, KP], U8, name=f"w1_sc{a}{b}", align_bytes=64)

        def round_w1(copy, a, b, c0, m0, m1, t0=0, t1=PACK):
            raw = w1_raw[a, b, c0][:, :, PACK * m0 - c0 : PACK * m1 - c0]
            copy(
                w1_stage[a, b][:, t0:t1, m0:m1, :].rearrange("p t m j -> p m t j"),
                raw.rearrange("p j (m t) -> p m t j", t=PACK)[:, :, t0:t1, :],
            )

        def quantize_w1(a, b, t0, t1):
            nc.vector.quantize_mx(
                out=w1_codes[a, b][:, P * t0 : P * t1].bitcast(FP8X4),
                scales=w1_sc[a, b][:, P * t0 : P * t1],
                in_=w1_stage[a, b][:, t0:t1, :, :].rearrange("p t m j -> p (t m j)"),
            )

        banks = {}

        def stage1_pass(a, b, t):
            first = (0, 2)[b]
            for half in range(2):
                cols = slice(NB * half, NB * (half + 1))
                if a == first:
                    banks[b, t, half] = psum.tile([P, NB], F32, name=f"bank{2 * t + half}")
                if a == 2:
                    c0 = KP * b + P * t
                    lhsT = w4_codes[:, 2 * c0 : 2 * (c0 + P)].bitcast(FP4X4)
                    lhsT_scale = w4_sc[:, c0 : c0 + P]
                else:
                    lhsT = w1_codes[a, b][:, P * t : P * (t + 1)].bitcast(FP8X4)
                    lhsT_scale = w1_sc[a, b][:, P * t : P * (t + 1)]
                nc.tensor.matmul_mx(
                    out=banks[b, t, half][:],
                    lhsT=lhsT,
                    lhsT_scale=lhsT_scale,
                    rhs=v_words[a][:, cols].bitcast(FP8X4),
                    rhs_scale=v_scales[SCALE_ROW[a] : P, cols],
                    start=(a == first),
                    stop=(a == 1),
                )

        feat = {}

        def tanh_plane(b, t):
            feat[b, t] = hpool.tile([P, S], F32, name="feat")
            for half in range(2):
                nc.scalar.activation(feat[b, t][:, NB * half : NB * (half + 1)], banks[b, t, half][:], ACT.Tanh)

        gather_tab(0)
        load_w1(0, 1, 0, KP, "tab_sb0")
        nc.vector.tensor_copy(v_scales[:], tabsc_sb[:].indirect(offs_sb[:]))
        load_w1(1, 1, 0, KP, "tabsc_sb")
        new_w1(0, 0)
        round_w1(nc.scalar.copy, 0, 0, 0, 0, P)
        quantize_w1(0, 0, 0, PACK)
        for t in range(PACK):
            stage1_pass(0, 0, t)
        gather_tab(2)
        w4_sc = held([P, H], U8, "w4_sc", "tab_sb2")
        nc.vector.tensor_copy(
            w4_sc[:].rearrange("p (b t m) -> p b t m", b=2, t=PACK),
            w4sc_raw[:].rearrange("p (b m t) -> p b t m", b=2, t=PACK),
        )
        for t in range(PACK):
            stage1_pass(2, 0, t)
        gather_tab(1)
        row_sb = held([P, NP], F32, "row_sb", "tab_sb1")
        nc.sync.dma_start(out=row_sb[:], in_=row.partition_broadcast(P))
        col_sb = held([P, NP // P], F32, "col_sb", "w4sc_raw")
        with nc.allow_non_contiguous_dma(reason="one factor for each output row"):
            nc.sync.dma_start(out=col_sb[:], in_=col.rearrange("(i p) -> p i", p=P))
        new_w1(1, 0)
        round_w1(nc.scalar.copy, 1, 0, 0, 0, 64)
        round_w1(nc.vector.tensor_copy, 1, 0, KP // 2, 64, P, 0, 1)
        quantize_w1(1, 0, 0, 1)
        round_w1(nc.vector.tensor_copy, 1, 0, KP // 2, 64, P, 1, PACK)
        quantize_w1(1, 0, 1, PACK)
        for t in range(PACK):
            stage1_pass(1, 0, t)
            tanh_plane(0, t)
        for b in range(2):
            for t in range(PACK):
                nc.scalar.copy(wide2[b, t][:], fac2[:, b, t : t + 1].to_broadcast([P, NP]))
            nc.scalar.copy(wide1[b][:], fac1[:, b, :].unsqueeze(2).to_broadcast([P, PACK, NP // 2]))

        x1_planes = {}
        x2_planes = {}

        def gather_x1(b, t, m0, n, tag):
            if t == 0:
                x1_planes[b, m0] = held([P, PACK, n], F32, f"x1_planes{b}_{m0}", tag)
            offsets = pos1_sb[:, m0 // 16 : (m0 + n) // 16]
            nc.vector.tensor_tensor(
                x1_planes[b, m0][:, t, :], feat[b, t][:].indirect(offsets), wide1[b][:, t, 0:n], ALU.mult
            )

        y_tiles = {}

        def gather_x2(b, t):
            y_tiles[b, t] = held([P, NP], F32, f"y_tile{b}{t}", "w1_stage0" if (b, t) == (0, 3) else f"y_tile{t}")
            nc.vector.tensor_tensor(y_tiles[b, t][:], feat[b, t][:].indirect(pos2_sb[:]), wide2[b, t][:], ALU.mult)

        def leaky_x2(b, t):
            if b not in x2_planes:
                x2_planes[b] = held([P, PACK, NP], BF16, f"x2_planes{b}", ("x2_planes0", "wide2_12")[b])
            y = y_tiles[b, t]
            nc.vector.scalar_tensor_tensor(
                x2_planes[b][:, t, :], y[:], slope_sb[:, b, t : t + 1], y[:], ALU.mult, ALU.max
            )

        x_codes = {}
        x_sc = {}
        x_stage = {}

        def weave(shares, key, planes, tag):
            n = planes.shape[2]
            x_stage[key] = held([P, n, PACK], BF16, "x_stage%s%d%d" % key, tag)
            for copy, c0, c1 in shares:
                copy(
                    x_stage[key][:, c0:c1, :].rearrange("p (c i) t -> p c t i", i=2),
                    planes[:, :, c0:c1].rearrange("p t (c i) -> p c t i", i=2),
                )

        def quantize_x(key):
            n = x_stage[key].shape[1]
            x_codes[key] = keep.tile([P, n], U32, name="x_codes%s%d%d" % key, align_bytes=64)
            x_sc[key] = keep.tile([P, n], U8, name="x_sc%s%d%d" % key, align_bytes=64)
            nc.vector.quantize_mx(
                out=x_codes[key][:].bitcast(FP8X4),
                scales=x_sc[key][:],
                in_=x_stage[key][:].rearrange("p n t -> p (n t)"),
            )

        for a in range(2):
            new_w1(a, 1)
            round_w1(nc.scalar.copy, a, 1, 0, 0, P)
        for t in range(PACK):
            if t == PACK - 1:
                quantize_w1(0, 1, 0, PACK)
            gather_x2(0, t)
            gather_x1(0, t, 0, 256, None)
            leaky_x2(0, t)
        quantize_w1(1, 1, 0, PACK)
        for t in range(PACK):
            gather_x1(0, t, 256, 256, "w1_stage1")
        for a in (2, 0, 1):
            for t in range(PACK):
                stage1_pass(a, 1, t)
                if a == 1:
                    tanh_plane(1, t)
        weave([(nc.scalar.copy, 0, NP // 2)], ("a", 0, 0), x1_planes[0, 0], "stage_a0")
        weave([(nc.scalar.copy, 0, NP)], ("b", 0, 0), x2_planes[0], "w1_codes11")
        weave([(nc.scalar.copy, 0, NP // 2)], ("a", 0, 1), x1_planes[0, 256], "w1_sc11")
        for t in range(PACK - 1):
            gather_x2(1, t)
        for t in range(PACK - 1):
            leaky_x2(1, t)
        gather_x2(1, PACK - 1)
        gather_x1(1, 0, 0, 256, "wide2_13")
        leaky_x2(1, PACK - 1)
        weave([(nc.scalar.copy, 0, NP)], ("b", 1, 0), x2_planes[1], "stage_b1")
        for t in range(1, PACK):
            gather_x1(1, t, 0, 256, None)
        quantize_x(("a", 0, 0))
        quantize_x(("b", 0, 0))
        quantize_x(("a", 0, 1))
        quantize_x(("b", 1, 0))
        weave([(nc.scalar.copy, 0, NP // 2)], ("a", 1, 0), x1_planes[1, 0], "stage_a1")
        for t in range(PACK):
            gather_x1(1, t, 256, P, "stage_b1")
        quantize_x(("a", 1, 0))
        weave([(nc.scalar.copy, 0, P)], ("a", 1, 2), x1_planes[1, 256], None)
        for t in range(PACK):
            gather_x1(1, t, 384, P, "stage_a1")
        quantize_x(("a", 1, 2))
        weave([(nc.vector.tensor_copy, 0, P)], ("a", 1, 3), x1_planes[1, 384], None)

        scores = [psum.tile([P, NP], F32, name=f"bank{i}") for i in range(NP // P)]

        def stage2_pass(b, i):
            key, c0 = (("a", b, i // 2), P * (i % 2)) if b == 0 or i < 2 else (("a", b, i), 0)
            nc.tensor.matmul_mx(
                out=scores[i][:],
                lhsT=x_codes[key][:, c0 : c0 + P].bitcast(FP8X4),
                lhsT_scale=x_sc[key][:, c0 : c0 + P],
                rhs=x_codes["b", b, 0][:].bitcast(FP8X4),
                rhs_scale=x_sc["b", b, 0][:],
                start=(b == 0),
                stop=(b == 1),
            )

        def finish(i, j0, j1):
            logits = hpool.tile([P, j1 - j0], F32, name="logits")
            nc.vector.tensor_tensor(logits[:], scores[i][:, j0:j1], row_sb[:, j0:j1], ALU.add)
            prob = hpool.tile([P, j1 - j0], F32, name="prob")
            nc.scalar.activation(prob[:], logits[:], ACT.Sigmoid)
            result = hpool.tile([P, j1 - j0], F32, name="result")
            if i == 0:
                nc.scalar.activation(result[:], prob[:], ACT.Copy, scale=col_sb[:, i : i + 1])
            else:
                nc.vector.tensor_scalar(result[:], prob[:], col_sb[:, i : i + 1], None, ALU.mult)
            nc.sync.dma_start(out=out[P * i : P * (i + 1), j0:j1], in_=result[:])

        for i in range(NP // P):
            stage2_pass(0, i)
        for i in range(NP // P - 1):
            stage2_pass(1, i)
        finish(0, 0, NP)
        quantize_x(("a", 1, 3))
        stage2_pass(1, 3)
        finish(1, 0, NP)
        finish(2, 0, NP)
        finish(3, 0, NP // 2)
        finish(3, NP // 2, NP)
